import numpy as np
import ml_dtypes


def mxq(x, axis, fmt="e4m3"):
    dtype, down = {"e4m3": (ml_dtypes.float8_e4m3fn, 7), "e5m2": (ml_dtypes.float8_e5m2, 14)}[fmt]
    v = np.moveaxis(np.asarray(x, np.float32).astype(ml_dtypes.bfloat16).astype(np.float64), axis, -1)
    blocks = v.reshape(v.shape[:-1] + (-1, 32))
    amax = np.abs(blocks).max(-1, keepdims=True)
    byte = np.maximum(np.where(amax > 0, np.frexp(amax)[1] - 1 + 127, 0) - down, 1)
    scale = np.exp2(byte - 127.0)
    codes = (blocks / scale).astype(np.float32).astype(dtype).astype(np.float64)
    return np.moveaxis((codes * scale).reshape(v.shape), -1, axis)


WIDE = False


def mx_kscale(k):
    if not WIDE:
        return np.ones(k)
    levels = np.array([10, -10, 5, -5, 0])
    if k % 512:
        return np.exp2(np.random.permutation(np.resize(levels, k // 32))).repeat(32)
    a = np.empty((k // 512, 16))
    for p in range(k // 512):
        a[p, :8] = np.random.permutation(np.resize(levels, 8))
        for g in range(8):
            far = levels[np.abs(levels - a[p, g]) >= 10]
            a[p, g + 8] = far[np.random.randint(len(far))]
    return np.exp2(a.ravel()).repeat(32)


def f64(x):
    return np.asarray(x).astype(np.float64)


def striped(idx):
    return np.tile(idx.reshape(-1, 16).T, (8, 1)).astype(np.uint16)


def unstriped(offs):
    return offs[:16].T.reshape(-1).astype(np.int64)


E2M1 = np.array([0.0, 0.5, 1.0, 1.5, 2.0, 3.0, 4.0, 6.0, -0.0, -0.5, -1.0, -1.5, -2.0, -3.0, -4.0, -6.0])


def pack_weight(w, fmt):
    k, n = w.shape
    w = f64(np.asarray(w, np.float32).astype(ml_dtypes.bfloat16)).reshape(k // 32, 32, n)
    amax = np.abs(w).max(1)
    if fmt == "e4m3":
        byte = np.frexp(amax)[1] - 1 + 127 - 7
    else:
        mant, ex = np.frexp(amax / 6.0)
        byte = np.where(mant > 0.5, ex, ex - 1) + 127
    byte = np.clip(np.where(amax > 0, byte, 1), 1, 254)
    scaled = (w * np.exp2(127.0 - byte)[:, None, :]).reshape(k, n).astype(np.float32)
    by_word = np.ascontiguousarray(scaled.reshape(k // 512, 128, 4, n).transpose(0, 1, 3, 2))
    if fmt == "e4m3":
        words = by_word.astype(ml_dtypes.float8_e4m3fn).view(np.uint8)
    else:
        c = by_word.astype(ml_dtypes.float4_e2m1fn).view(np.uint8) & 0xF
        words = (c[..., 0::2] | (c[..., 1::2] << 4)).reshape(k // 512, 128, 2 * n)
    return np.ascontiguousarray(words), np.ascontiguousarray(byte.astype(np.uint8).reshape(k // 512, 16, n))


def unpack_weight(words, scales, fmt):
    g, _, n = scales.shape
    words = np.ascontiguousarray(words).reshape(g, 128, n, -1)
    if fmt == "e4m3":
        vals = words.view(ml_dtypes.float8_e4m3fn).astype(np.float64)
    else:
        nib = np.empty((g, 128, n, 4), np.uint8)
        nib[..., 0::2] = words & 0xF
        nib[..., 1::2] = words >> 4
        vals = E2M1[nib]
    vals = vals * np.repeat(np.exp2(scales.astype(np.float64) - 127.0), 8, axis=1)[..., None]
    return vals.transpose(0, 1, 3, 2).reshape(g * 512, n)


def gelu(v):
    return 0.5 * v * (1.0 + np.tanh(np.sqrt(2.0 / np.pi) * (v + 0.044715 * v**3)))


K, KA, KB, T, H, S, T2, P, T3, S2 = 1536, 1024, 512, 4096, 1024, 1024, 2048, 512, 2048, 1024

def setup_inputs():
    n = np.random.standard_normal
    s = mx_kscale(K)[:, None]
    u = mx_kscale(H)[:, None]
    tab_words, tab_scales = pack_weight(n((K, T)) * s, "e4m3")
    tab2_words, tab2_scales = pack_weight(n((H, T3)) * 1.6 / np.sqrt(H) / u, "e4m3")
    w4_words, w4_scales = pack_weight(n((KB, H)) * 2.0 / np.sqrt(K) / s[KA:], "e2m1")
    return {
        "tab_words": tab_words, "tab_scales": tab_scales,
        "tab2_words": tab2_words, "tab2_scales": tab2_scales,
        "w1": (n((KA, H)) * 2.0 / np.sqrt(K) / s[:KA]).astype(np.float32),
        "w4_words": w4_words, "w4_scales": w4_scales,
        "gain": (1.4 * np.exp(0.3 * n(H)) * u[:, 0]).astype(np.float32),
        "page0": (n((H, T2)) * u).astype(np.float32),
        "wgs": np.exp(0.3 * n((128, S))).astype(np.float32),
        "cand": n(S2).astype(np.float32),
        "offs": striped(np.random.permutation(T)[:S]),
        "offs2": striped(np.random.permutation(T3)[:S2]),
        "offs3": striped(np.random.permutation(T2)[:S]),
        "offs4": striped(np.random.permutation(T2)[:P]),
    }

def reference(tab_words, tab_scales, tab2_words, tab2_scales, w1, w4_words, w4_scales,
              gain, page0, wgs, cand, offs, offs2, offs3, offs4):
    v = unpack_weight(tab_words, tab_scales, "e4m3")[:, unstriped(offs)]
    v2 = unpack_weight(tab2_words, tab2_scales, "e4m3")[:, unstriped(offs2)]
    w4 = unpack_weight(w4_words, w4_scales, "e2m1")
    f = mxq(f64(w1), 0, "e4m3").T @ v[:KA] + w4.T @ v[KA:]
    h = f64(gain)[:, None] * np.tanh(f)
    page = f64(page0).copy()
    page[:, unstriped(offs3)] = np.tile(f64(wgs), (H // 128, 1)) * h
    x = np.abs(page[:, unstriped(offs4)])
    e = v2.T @ mxq(x, 0, "e4m3")
    return 1.0 / (1.0 + np.exp(-(e + f64(cand)[:, None])))

@@ -1,0 +1,328 @@
+from contextlib import ExitStack
+
+import concourse.mybir as mybir
+from concourse.masks import make_identity
+
+F32 = mybir.dt.float32
+BF16 = mybir.dt.bfloat16
+U32 = mybir.dt.uint32
+I32 = mybir.dt.int32
+U16 = mybir.dt.uint16
+U8 = mybir.dt.uint8
+FP8X4 = mybir.dt.float8_e4m3fn_x4
+FP4X4 = mybir.dt.float4_e2m1fn_x4
+ACT = mybir.ActivationFunctionType
+MULT = mybir.AluOpType.mult
+
+P = 128
+K, KA, T, H, S, T2, NQ, T3, S2 = 1536, 1024, 4096, 1024, 1024, 2048, 512, 2048, 1024
+FLOPS = 2 * K * H * S + 2 * H * S2 * NQ
+HALF = 512
+QH = 256
+EARLY_A0 = True
+
+
+def tile_list_edited_snippet_scores_kernel(
+    tc, tab_words, tab_scales, tab2_words, tab2_scales, w1, w4_words, w4_scales,
+    gain, page0, wgs, cand, offs, offs2, offs3, offs4, out,
+):
+    nc = tc.nc
+    with ExitStack() as ctx:
+        keep = ctx.enter_context(tc.tile_pool(name="keep", bufs=1))
+        ring = ctx.enter_context(tc.tile_pool(name="ring", bufs=2))
+        psum = ctx.enter_context(tc.psum_pool(name="psum", bufs=1))
+
+        def held(shape, dtype, name):
+            return keep.tile(shape, dtype, name=name, align_bytes=64)
+
+        def bank(b, shape):
+            return psum.tile(shape, F32, name="bank%d" % b, tag="bank%d" % b)
+
+        list1 = keep.tile([P, S // 16], U16, name="list1")
+        list2 = keep.tile([P, S2 // 16], U16, name="list2")
+        list3 = keep.tile([P, S // 16], U16, name="list3")
+        list4 = keep.tile([P, NQ // 16], U16, name="list4")
+
+        tabw = [held([P, T], U32, "tabw%d" % a) for a in range(3)]
+        tabs = held([P, T], U8, "tabs")
+        tab2w = [held([P, T3], U32, "tab2w%d" % a) for a in range(2)]
+        tab2s = held([P, T3], U8, "tab2s")
+        w4w = held([P, 2 * H], U8, "w4w")
+        w4s = held([P, H], U8, "w4s")
+        w4w_d = held([P, H], U8, "w4w_d")
+        w4s_d = held([P, HALF], U8, "w4s_d")
+        vw = [held([P, S], U32, "vw%d" % a) for a in range(3)]
+        vs = held([P, S], U8, "vs")
+        v2w = [held([P, S2], U32, "v2w%d" % a) for a in range(2)]
+        v2s = held([P, S2], U8, "v2s")
+        wgs_n = held([P, S], F32, "wgs_n")
+        wgs_d = held([P, 4, S], F32, "wgs_d")
+        gain_n = held([P, 4], F32, "gain_n")
+        gain_d = held([P, 4], F32, "gain_d")
+        cand_t = held([P, 8], F32, "cand_t")
+        ident = held([P, P], F32, "ident")
+        x_turned = held([P, 4, HALF], BF16, "x_turned")
+        x_woven = [[held([P, QH, 4], BF16, "x_woven%d%d" % (b, h)) for h in range(2)] for b in range(2)]
+        x_codes = [[held([P, QH], U32, "x_codes%d%d" % (b, h)) for h in range(2)] for b in range(2)]
+        x_scales = [[held([P, QH], U8, "x_scales%d%d" % (b, h)) for h in range(2)] for b in range(2)]
+
+        def load_words(tile, words):
+            nc.sync.dma_start(out=tile[:].bitcast(I32), in_=words.rearrange("p t i -> p (t i)").bitcast(I32))
+
+        def load_w1(a, c0, width, tag):
+            raw = keep.tile([P, 4, width], F32, name="raw%d_%d" % (a, c0), tag=tag)
+            nc.sync.dma_start(
+                out=raw[:], in_=w1[512 * a : 512 * (a + 1), c0 : c0 + width].rearrange("(p j) c -> p j c", j=4))
+            return raw
+
+        def quantise_w1(raw, a, c0, width, dealt):
+            grouped = ring.tile([P, 4 * width], BF16, name="grouped", tag="grouped", align_bytes=64)
+            if dealt:
+                nc.scalar.copy(
+                    out=grouped[:].rearrange("p (t m j) -> p m t j", t=4, j=4),
+                    in_=raw[:].rearrange("p j (m t) -> p m t j", t=4))
+            else:
+                nc.scalar.copy(
+                    out=grouped[:].rearrange("p (c i j) -> p c j i", i=4, j=4),
+                    in_=raw[:].rearrange("p j (c i) -> p c j i", i=4))
+            codes = held([P, width], U32, "w1c%d_%d" % (a, c0))
+            scales = held([P, width], U8, "w1s%d_%d" % (a, c0))
+            nc.vector.quantize_mx(out=codes[:].bitcast(FP8X4), scales=scales[:], in_=grouped[:])
+            return codes, scales
+
+        def load_page(c):
+            page = ring.tile([P, T2], F32, name="page", tag="page", bufs=4)
+            if c < 4:
+                rows = page0[P * c : P * (c + 1), :]
+            else:
+                rows = page0[HALF:H, :].rearrange("(p t) s -> p t s", t=4)[:, c - 4, :]
+            nc.sync.dma_start(out=page[:], in_=rows)
+            return page
+
+        nc.vector.memset(tabs[:].bitcast(I32), 0)
+        nc.vector.memset(tab2s[:].bitcast(I32), 0)
+        nc.vector.memset(w4s[:].bitcast(I32), 0)
+        for q in range(4):
+            nc.gpsimd.dma_start(
+                out=tabs[32 * q + 4 : 32 * q + 12, :].bitcast(I32),
+                in_=tab_scales[0:2, 4 * q : 4 * q + 4, :].bitcast(I32))
+        with nc.allow_non_contiguous_dma(reason="one gain a partition"):
+            nc.gpsimd.dma_start(out=gain_n[:], in_=gain[0:HALF].rearrange("(c p) -> p c", p=P))
+        for q in range(4):
+            nc.gpsimd.dma_start(
+                out=tab2s[32 * q : 32 * q + 8, :].bitcast(I32),
+                in_=tab2_scales[0:2, 4 * q : 4 * q + 4, :].bitcast(I32))
+        make_identity(nc, ident[:])
+
+        pages = {}
+        raws = {}
+        load_words(tabw[0], tab_words[0])
+        nc.sync.dma_start(list1[:], offs)
+        for q in range(4):
+            nc.sync.dma_start(
+                out=tabs[32 * q : 32 * q + 4, :].bitcast(I32),
+                in_=tab_scales[2, 4 * q : 4 * q + 4, :].bitcast(I32))
+        load_words(tabw[1], tab_words[1])
+        nc.sync.dma_start(list2[:], offs2)
+        for a in range(2):
+            raws[a, 0] = load_w1(a, 0, 256, "rawd%d" % a)
+        nc.sync.dma_start(out=w4w[:].bitcast(I32), in_=w4_words[0].bitcast(I32))
+        load_words(tabw[2], tab_words[2])
+        for q in range(4):
+            nc.sync.dma_start(
+                out=w4s[32 * q : 32 * q + 4, :].bitcast(I32),
+                in_=w4_scales[0, 4 * q : 4 * q + 4, :].bitcast(I32))
+        nc.sync.dma_start(list3[:], offs3)
+        nc.sync.dma_start(out=wgs_n[:], in_=wgs)
+        pages[0] = load_page(0)
+        for a in range(2):
+            raws[a, 256] = load_w1(a, 256, 256, "rawm%d" % a)
+        nc.sync.dma_start(list4[:], offs4)
+        raws[0, 512] = load_w1(0, 512, 512, "rawd0")
+        pages[1] = load_page(1)
+        raws[1, 512] = load_w1(1, 512, 512, "rawd1")
+        pages[2] = load_page(2)
+        nc.sync.dma_start(out=gain_d[:], in_=gain[HALF:H].rearrange("(p t) -> p t", t=4))
+        for g in (0, 2, 1, 3):
+            nc.sync.dma_start(
+                out=wgs_d[32 * g : 32 * (g + 1), :, :], in_=wgs.rearrange("(i t) j -> i t j", t=4))
+        pages[3] = load_page(3)
+        with nc.allow_non_contiguous_dma(reason="one offset a partition"):
+            nc.sync.dma_start(out=cand_t[:], in_=cand.rearrange("(c p) -> p c", p=P))
+
+        nc.vector.tensor_copy(vw[0][:], tabw[0][:].indirect(list1[:]))
+        nc.vector.tensor_copy(vs[:], tabs[:].indirect(list1[:]))
+        nc.vector.tensor_copy(vw[1][:], tabw[1][:].indirect(list1[:]))
+        nc.vector.tensor_copy(v2s[:], tab2s[:].indirect(list2[:]))
+        w1q = {}
+        for a in range(2):
+            w1q[a, 0] = quantise_w1(raws[a, 0], a, 0, 256, False)
+        for jh in range(2):
+            nc.vector.tensor_copy(
+                vw[2][:, HALF * jh : HALF * (jh + 1)], tabw[2][:].indirect(list1[:, 32 * jh : 32 * (jh + 1)]))
+        nc.vector.tensor_copy(
+            out=w4w_d[:].rearrange("p (t m e) -> p m t e", t=4, e=2),
+            in_=w4w[:, H : 2 * H].rearrange("p (m t e) -> p m t e", t=4, e=2))
+        nc.vector.tensor_copy(
+            out=w4s_d[:].rearrange("p (t m) -> p m t", t=4),
+            in_=w4s[:, HALF:H].rearrange("p (m t) -> p m t", t=4))
+
+        def stage1(c):
+            if c < 4:
+                c0, col = 256 * (c // 2), P * (c % 2)
+                w4c, w4sc = w4w[:, 2 * P * c : 2 * P * (c + 1)], w4s[:, P * c : P * (c + 1)]
+                wg_src, gain_col = wgs_n[:], gain_n[:, c : c + 1]
+            else:
+                t = c - 4
+                c0, col = HALF, P * t
+                w4c, w4sc = w4w_d[:, 2 * P * t : 2 * P * (t + 1)], w4s_d[:, P * t : P * (t + 1)]
+                wg_src, gain_col = wgs_d[:, t, :], gain_d[:, t : t + 1]
+            th = ring.tile([P, S], F32, name="th", tag="th")
+            wg = ring.tile([P, S], F32, name="wg", tag="wg")
+            accs = [bank(2 * (c % 2) + jh, [P, HALF]) for jh in range(2)]
+            for a in range(3):
+                for jh in range(2):
+                    cols = slice(HALF * jh, HALF * (jh + 1))
+                    if a < 2:
+                        codes, scales = w1q[a, c0]
+                        lhs, lhs_s = codes[:, col : col + P].bitcast(FP8X4), scales[:, col : col + P]
+                        plane = 4 * (a + 1)
+                    else:
+                        lhs, lhs_s = w4c.bitcast(FP4X4), w4sc
+                        plane = 0
+                    nc.tensor.matmul_mx(
+                        out=accs[jh][:], lhsT=lhs, lhsT_scale=lhs_s,
+                        rhs=vw[a][:, cols].bitcast(FP8X4), rhs_scale=vs[plane:P, cols],
+                        start=(a == 0), stop=(a == 2))
+            if c == 0:
+                for jh in range(2):
+                    cols = slice(HALF * jh, HALF * (jh + 1))
+                    nc.scalar.activation(out=th[:, cols], in_=accs[jh][:], func=ACT.Tanh)
+                    nc.scalar.activation(out=wg[:, cols], in_=wg_src[:, cols], func=ACT.Copy, scale=gain_col)
+            else:
+                for jh in range(2):
+                    cols = slice(HALF * jh, HALF * (jh + 1))
+                    nc.scalar.activation(out=th[:, cols], in_=accs[jh][:], func=ACT.Tanh)
+                nc.scalar.activation(out=wg[:], in_=wg_src, func=ACT.Copy, scale=gain_col)
+            return th, wg
+
+        def scatter(c, th, wg):
+            page = pages[c]
+            if c == 0:
+                for jh in range(2):
+                    cols = slice(HALF * jh, HALF * (jh + 1))
+                    nc.vector.tensor_tensor(
+                        page[:].indirect(list3[:, 32 * jh : 32 * (jh + 1)]), th[:, cols], wg[:, cols], MULT)
+            else:
+                nc.vector.tensor_tensor(page[:].indirect(list3[:]), th[:], wg[:], MULT)
+
+        def fetch(c):
+            page = pages[c]
+            picked = ring.tile([P, NQ], F32, name="picked", tag="picked", bufs=3)
+            if c < 7:
+                nc.vector.tensor_copy(picked[:], page[:].indirect(list4[:]))
+            else:
+                for h in range(2):
+                    nc.vector.tensor_copy(
+                        picked[:, QH * h : QH * (h + 1)], page[:].indirect(list4[:, 16 * h : 16 * (h + 1)]))
+            if c < 4:
+                turned = bank(4 + c % 2, [P, 4, P])
+                for nb in range(4):
+                    nc.tensor.transpose(turned[:, nb, :], picked[:, P * nb : P * (nb + 1)], ident[:])
+                nc.scalar.activation(out=x_turned[:, :, P * c : P * (c + 1)], in_=turned[:], func=ACT.Abs)
+            else:
+                for h in range(2):
+                    nc.scalar.activation(
+                        out=x_woven[1][h][:, :, c - 4], in_=picked[:, QH * h : QH * (h + 1)], func=ACT.Abs)
+
+        def turn_back():
+            words = x_turned[:].bitcast(F32)
+            for h in range(2):
+                back = bank(6 + h, [P, 2, 2, P])
+                for i in range(2):
+                    for u in range(2):
+                        nc.tensor.transpose(back[:, i, u, :], words[:, 2 * h + i, u : 256 : 2], ident[:])
+                nc.scalar.copy(
+                    out=x_woven[0][h][:].rearrange("p n t -> p (n t)").bitcast(F32).rearrange(
+                        "p (i n u) -> p i n u", i=2, u=2),
+                    in_=back[:].rearrange("p i u n -> p i n u"))
+
+        def quantise_x(b, h):
+            nc.vector.quantize_mx(
+                out=x_codes[b][h][:].bitcast(FP8X4), scales=x_scales[b][h][:],
+                in_=x_woven[b][h][:].rearrange("p n t -> p (n t)"))
+
+        def gather_v2(a, k):
+            cols = slice(QH * k, QH * (k + 1))
+            nc.vector.tensor_copy(v2w[a][:, cols], tab2w[a][:].indirect(list2[:, 16 * k : 16 * (k + 1)]))
+
+        def score_pass(acc, b, h, k):
+            for i in range(2):
+                cols = slice(P * (2 * k + i), P * (2 * k + i + 1))
+                nc.tensor.matmul_mx(
+                    out=acc[:, i, :], lhsT=v2w[b][:, cols].bitcast(FP8X4), lhsT_scale=v2s[4 * b : P, cols],
+                    rhs=x_codes[b][h][:].bitcast(FP8X4), rhs_scale=x_scales[b][h][:],
+                    start=(b == 0 and i == 0), stop=(b == 1 and i == 1))
+
+        made = {0: stage1(0), 1: stage1(1)}
+        for c in range(8):
+            scatter(c, *made[c])
+            if c == 0:
+                for a in range(2):
+                    w1q[a, 256] = quantise_w1(raws[a, 256], a, 256, 256, False)
+            if c == 1:
+                for a in range(2):
+                    w1q[a, HALF] = quantise_w1(raws[a, HALF], a, HALF, HALF, True)
+            if c + 2 < 8:
+                made[c + 2] = stage1(c + 2)
+            if c == 4:
+                for h in range(2):
+                    quantise_x(0, h)
+            fetch(c)
+            if c == 3:
+                turn_back()
+            if c + 4 < 8:
+                pages[c + 4] = load_page(c + 4)
+            if EARLY_A0 and c == 0:
+                load_words(tab2w[0], tab2_words[0])
+            if EARLY_A0 and c == 5:
+                nc.vector.tensor_copy(v2w[0][:], tab2w[0][:].indirect(list2[:]))
+            if c == 3:
+                if not EARLY_A0:
+                    load_words(tab2w[0], tab2_words[0])
+                load_words(tab2w[1], tab2_words[1])
+
+        accs = {}
+        if EARLY_A0:
+            for h in range(2):
+                for k in range(4):
+                    accs[h, k] = bank(4 * (1 - h) + k, [P, 2, QH])
+                    score_pass(accs[h, k], 0, h, k)
+        out_tags = [(ring, "th"), (ring, "wg"), (keep, "rawd0"), (keep, "rawd1"),
+                    (ring, "th"), (ring, "wg"), (keep, "rawm0"), (keep, "rawm1")]
+
+        def finish(h, k, n):
+            pool, tag = out_tags[n]
+            res = pool.tile([P, 2, QH], F32, name="res", tag=tag)
+            for i in range(2):
+                nc.scalar.activation(
+                    out=res[:, i, :], in_=accs[h, k][:, i, :], func=ACT.Sigmoid,
+                    bias=cand_t[:, 2 * k + i : 2 * k + i + 1])
+            nc.sync.dma_start(
+                out=out[2 * P * k : 2 * P * (k + 1), QH * h : QH * (h + 1)].rearrange("(i p) n -> p i n", p=P),
+                in_=res[:])
+
+        n = 0
+        for k in range(4):
+            if not EARLY_A0:
+                gather_v2(0, k)
+            gather_v2(1, k)
+            for h in range(2):
+                if k == 0:
+                    quantise_x(1, h)
+                if not EARLY_A0:
+                    accs[h, k] = bank(4 * (1 - h) + k, [P, 2, QH])
+                    score_pass(accs[h, k], 0, h, k)
+                score_pass(accs[h, k], 1, h, k)
+                finish(h, k, n)
+                n = n + 1

@@ -19,7 +19,6 @@ K, KA, T, H, S, T2, NQ, T3, S2 = 1536, 1024, 4096, 1024, 1024, 2048, 512, 2048, 
 FLOPS = 2 * K * H * S + 2 * H * S2 * NQ
 HALF = 512
 QH = 256
-EARLY_A0 = True
 
 
 def tile_list_edited_snippet_scores_kernel(
@@ -53,7 +52,7 @@ def tile_list_edited_snippet_scores_kernel(
         w4s_d = held([P, HALF], U8, "w4s_d")
         vw = [held([P, S], U32, "vw%d" % a) for a in range(3)]
         vs = held([P, S], U8, "vs")
-        v2w = [held([P, S2], U32, "v2w%d" % a) for a in range(2)]
+        v2w = {}
         v2s = held([P, S2], U8, "v2s")
         wgs_n = held([P, S], F32, "wgs_n")
         wgs_d = held([P, 4, S], F32, "wgs_d")
@@ -62,22 +61,23 @@ def tile_list_edited_snippet_scores_kernel(
         cand_t = held([P, 8], F32, "cand_t")
         ident = held([P, P], F32, "ident")
         x_turned = held([P, 4, HALF], BF16, "x_turned")
-        x_woven = [[held([P, QH, 4], BF16, "x_woven%d%d" % (b, h)) for h in range(2)] for b in range(2)]
-        x_codes = [[held([P, QH], U32, "x_codes%d%d" % (b, h)) for h in range(2)] for b in range(2)]
+        x_woven = [[keep.tile([P, QH, 4], BF16, name="x_woven", tag="x_woven%d%d" % (b, h), align_bytes=64)
+                    for h in range(2)] for b in range(2)]
+        x_codes = {}
         x_scales = [[held([P, QH], U8, "x_scales%d%d" % (b, h)) for h in range(2)] for b in range(2)]
 
         def load_words(tile, words):
             nc.sync.dma_start(out=tile[:].bitcast(I32), in_=words.rearrange("p t i -> p (t i)").bitcast(I32))
 
         def load_w1(a, c0, width, tag):
-            raw = keep.tile([P, 4, width], F32, name="raw%d_%d" % (a, c0), tag=tag)
+            raw = keep.tile([P, 4, width], F32, name="raw%d_%d" % (a, c0), tag=tag, align_bytes=64)
             nc.sync.dma_start(
                 out=raw[:], in_=w1[512 * a : 512 * (a + 1), c0 : c0 + width].rearrange("(p j) c -> p j c", j=4))
             return raw
 
         def quantise_w1(raw, a, c0, width, dealt):
             grouped = ring.tile([P, 4 * width], BF16, name="grouped", tag="grouped", align_bytes=64)
-            if dealt:
+            if dealt is not None:
                 nc.scalar.copy(
                     out=grouped[:].rearrange("p (t m j) -> p m t j", t=4, j=4),
                     in_=raw[:].rearrange("p j (m t) -> p m t j", t=4))
@@ -85,9 +85,12 @@ def tile_list_edited_snippet_scores_kernel(
                 nc.scalar.copy(
                     out=grouped[:].rearrange("p (c i j) -> p c j i", i=4, j=4),
                     in_=raw[:].rearrange("p j (c i) -> p c j i", i=4))
-            codes = held([P, width], U32, "w1c%d_%d" % (a, c0))
+            if dealt is not None:
+                codes = dealt
+            else:
+                codes = held([P, width], U32, "w1c%d_%d" % (a, c0))[:]
             scales = held([P, width], U8, "w1s%d_%d" % (a, c0))
-            nc.vector.quantize_mx(out=codes[:].bitcast(FP8X4), scales=scales[:], in_=grouped[:])
+            nc.vector.quantize_mx(out=codes.bitcast(FP8X4), scales=scales[:], in_=grouped[:])
             return codes, scales
 
         def load_page(c):
@@ -100,46 +103,46 @@ def tile_list_edited_snippet_scores_kernel(
             return page
 
         nc.vector.memset(tabs[:].bitcast(I32), 0)
-        nc.vector.memset(tab2s[:].bitcast(I32), 0)
         nc.vector.memset(w4s[:].bitcast(I32), 0)
+        nc.vector.memset(tab2s[:].bitcast(I32), 0)
         for q in range(4):
             nc.gpsimd.dma_start(
                 out=tabs[32 * q + 4 : 32 * q + 12, :].bitcast(I32),
                 in_=tab_scales[0:2, 4 * q : 4 * q + 4, :].bitcast(I32))
-        with nc.allow_non_contiguous_dma(reason="one gain a partition"):
-            nc.gpsimd.dma_start(out=gain_n[:], in_=gain[0:HALF].rearrange("(c p) -> p c", p=P))
-        for q in range(4):
-            nc.gpsimd.dma_start(
-                out=tab2s[32 * q : 32 * q + 8, :].bitcast(I32),
-                in_=tab2_scales[0:2, 4 * q : 4 * q + 4, :].bitcast(I32))
         make_identity(nc, ident[:])
 
         pages = {}
         raws = {}
         load_words(tabw[0], tab_words[0])
         nc.sync.dma_start(list1[:], offs)
+        for a in range(2):
+            raws[a, 0] = load_w1(a, 0, 256, "rawd%d" % a)
         for q in range(4):
             nc.sync.dma_start(
                 out=tabs[32 * q : 32 * q + 4, :].bitcast(I32),
                 in_=tab_scales[2, 4 * q : 4 * q + 4, :].bitcast(I32))
         load_words(tabw[1], tab_words[1])
-        nc.sync.dma_start(list2[:], offs2)
-        for a in range(2):
-            raws[a, 0] = load_w1(a, 0, 256, "rawd%d" % a)
         nc.sync.dma_start(out=w4w[:].bitcast(I32), in_=w4_words[0].bitcast(I32))
-        load_words(tabw[2], tab_words[2])
+        nc.sync.dma_start(list3[:], offs3)
         for q in range(4):
             nc.sync.dma_start(
                 out=w4s[32 * q : 32 * q + 4, :].bitcast(I32),
                 in_=w4_scales[0, 4 * q : 4 * q + 4, :].bitcast(I32))
-        nc.sync.dma_start(list3[:], offs3)
+        load_words(tabw[2], tab_words[2])
+        with nc.allow_non_contiguous_dma(reason="one gain a partition"):
+            nc.sync.dma_start(out=gain_n[:], in_=gain[0:HALF].rearrange("(c p) -> p c", p=P))
         nc.sync.dma_start(out=wgs_n[:], in_=wgs)
         pages[0] = load_page(0)
         for a in range(2):
             raws[a, 256] = load_w1(a, 256, 256, "rawm%d" % a)
         nc.sync.dma_start(list4[:], offs4)
-        raws[0, 512] = load_w1(0, 512, 512, "rawd0")
         pages[1] = load_page(1)
+        nc.sync.dma_start(list2[:], offs2)
+        for q in range(4):
+            nc.sync.dma_start(
+                out=tab2s[32 * q : 32 * q + 8, :].bitcast(I32),
+                in_=tab2_scales[0:2, 4 * q : 4 * q + 4, :].bitcast(I32))
+        raws[0, 512] = load_w1(0, 512, 512, "rawd0")
         raws[1, 512] = load_w1(1, 512, 512, "rawd1")
         pages[2] = load_page(2)
         nc.sync.dma_start(out=gain_d[:], in_=gain[HALF:H].rearrange("(p t) -> p t", t=4))
@@ -151,12 +154,11 @@ def tile_list_edited_snippet_scores_kernel(
             nc.sync.dma_start(out=cand_t[:], in_=cand.rearrange("(c p) -> p c", p=P))
 
         nc.vector.tensor_copy(vw[0][:], tabw[0][:].indirect(list1[:]))
-        nc.vector.tensor_copy(vs[:], tabs[:].indirect(list1[:]))
-        nc.vector.tensor_copy(vw[1][:], tabw[1][:].indirect(list1[:]))
-        nc.vector.tensor_copy(v2s[:], tab2s[:].indirect(list2[:]))
         w1q = {}
         for a in range(2):
-            w1q[a, 0] = quantise_w1(raws[a, 0], a, 0, 256, False)
+            w1q[a, 0] = quantise_w1(raws[a, 0], a, 0, 256, None)
+        nc.vector.tensor_copy(vs[:], tabs[:].indirect(list1[:]))
+        nc.vector.tensor_copy(vw[1][:], tabw[1][:].indirect(list1[:]))
         for jh in range(2):
             nc.vector.tensor_copy(
                 vw[2][:, HALF * jh : HALF * (jh + 1)], tabw[2][:].indirect(list1[:, 32 * jh : 32 * (jh + 1)]))
@@ -177,8 +179,8 @@ def tile_list_edited_snippet_scores_kernel(
                 c0, col = HALF, P * t
                 w4c, w4sc = w4w_d[:, 2 * P * t : 2 * P * (t + 1)], w4s_d[:, P * t : P * (t + 1)]
                 wg_src, gain_col = wgs_d[:, t, :], gain_d[:, t : t + 1]
-            th = ring.tile([P, S], F32, name="th", tag="th")
-            wg = ring.tile([P, S], F32, name="wg", tag="wg")
+            th = keep.tile([P, S], F32, name="th", tag="th%d" % (c % 2), align_bytes=64)
+            wg = keep.tile([P, S], F32, name="wg", tag="wg_%d" % c if c in (2, 4) else "wg%d" % (c % 2), align_bytes=64)
             accs = [bank(2 * (c % 2) + jh, [P, HALF]) for jh in range(2)]
             for a in range(3):
                 for jh in range(2):
@@ -249,19 +251,20 @@ def tile_list_edited_snippet_scores_kernel(
 
         def quantise_x(b, h):
             nc.vector.quantize_mx(
-                out=x_codes[b][h][:].bitcast(FP8X4), scales=x_scales[b][h][:],
+                out=x_codes[b, h].bitcast(FP8X4), scales=x_scales[b][h][:],
                 in_=x_woven[b][h][:].rearrange("p n t -> p (n t)"))
 
-        def gather_v2(a, k):
-            cols = slice(QH * k, QH * (k + 1))
-            nc.vector.tensor_copy(v2w[a][:, cols], tab2w[a][:].indirect(list2[:, 16 * k : 16 * (k + 1)]))
+        def gather_v2(a, k, dst):
+            nc.vector.tensor_copy(dst, tab2w[a][:].indirect(list2[:, 16 * k : 16 * (k + 1)]))
+            v2w[a, k] = dst
 
         def score_pass(acc, b, h, k):
             for i in range(2):
                 cols = slice(P * (2 * k + i), P * (2 * k + i + 1))
                 nc.tensor.matmul_mx(
-                    out=acc[:, i, :], lhsT=v2w[b][:, cols].bitcast(FP8X4), lhsT_scale=v2s[4 * b : P, cols],
-                    rhs=x_codes[b][h][:].bitcast(FP8X4), rhs_scale=x_scales[b][h][:],
+                    out=acc[:, i, :], lhsT=v2w[b, k][:, P * i : P * (i + 1)].bitcast(FP8X4),
+                    lhsT_scale=v2s[4 * b : P, cols],
+                    rhs=x_codes[b, h].bitcast(FP8X4), rhs_scale=x_scales[b][h][:],
                     start=(b == 0 and i == 0), stop=(b == 1 and i == 1))
 
         made = {0: stage1(0), 1: stage1(1)}
@@ -269,41 +272,47 @@ def tile_list_edited_snippet_scores_kernel(
             scatter(c, *made[c])
             if c == 0:
                 for a in range(2):
-                    w1q[a, 256] = quantise_w1(raws[a, 256], a, 256, 256, False)
+                    w1q[a, 256] = quantise_w1(raws[a, 256], a, 256, 256, None)
             if c == 1:
+                nc.vector.tensor_copy(v2s[:], tab2s[:].indirect(list2[:]))
+            if c == 2:
+                dealt_codes = keep.tile([P, 2 * HALF], U32, name="dealt_codes", tag="wg_2", align_bytes=64)
                 for a in range(2):
-                    w1q[a, HALF] = quantise_w1(raws[a, HALF], a, HALF, HALF, True)
+                    w1q[a, HALF] = quantise_w1(
+                        raws[a, HALF], a, HALF, HALF, dealt_codes[:, HALF * a : HALF * (a + 1)])
             if c + 2 < 8:
                 made[c + 2] = stage1(c + 2)
             if c == 4:
+                codes0 = keep.tile([P, NQ], U32, name="codes0", tag="wg_4", align_bytes=64)
                 for h in range(2):
+                    x_codes[0, h] = codes0[:, QH * h : QH * (h + 1)]
                     quantise_x(0, h)
             fetch(c)
             if c == 3:
                 turn_back()
             if c + 4 < 8:
                 pages[c + 4] = load_page(c + 4)
-            if EARLY_A0 and c == 0:
+            if c == 0:
                 load_words(tab2w[0], tab2_words[0])
-            if EARLY_A0 and c == 5:
-                nc.vector.tensor_copy(v2w[0][:], tab2w[0][:].indirect(list2[:]))
-            if c == 3:
-                if not EARLY_A0:
-                    load_words(tab2w[0], tab2_words[0])
+            if c == 2:
                 load_words(tab2w[1], tab2_words[1])
+            if c == 5:
+                early = held([P, 2 * QH], U32, "v2_early")
+                nc.vector.tensor_copy(early[:], tab2w[0][:].indirect(list2[:, 0:32]))
+                for k in range(2):
+                    v2w[0, k] = early[:, QH * k : QH * (k + 1)]
 
         accs = {}
-        if EARLY_A0:
-            for h in range(2):
-                for k in range(4):
-                    accs[h, k] = bank(4 * (1 - h) + k, [P, 2, QH])
-                    score_pass(accs[h, k], 0, h, k)
-        out_tags = [(ring, "th"), (ring, "wg"), (keep, "rawd0"), (keep, "rawd1"),
-                    (ring, "th"), (ring, "wg"), (keep, "rawm0"), (keep, "rawm1")]
+        for h in range(2):
+            for k in range(2):
+                accs[h, k] = bank(4 + 2 * h + k, [P, 2, QH])
+                score_pass(accs[h, k], 0, h, k)
+        out_tags = [(keep, "th0"), (keep, "wg0"), (keep, "rawd0"), (keep, "rawd1"),
+                    (ring, "grouped"), (ring, "grouped"), (keep, "rawm0"), (keep, "rawm1")]
 
         def finish(h, k, n):
             pool, tag = out_tags[n]
-            res = pool.tile([P, 2, QH], F32, name="res", tag=tag)
+            res = pool.tile([P, 2, QH], F32, name="res", tag=tag, align_bytes=64)
             for i in range(2):
                 nc.scalar.activation(
                     out=res[:, i, :], in_=accs[h, k][:, i, :], func=ACT.Sigmoid,
@@ -312,17 +321,28 @@ def tile_list_edited_snippet_scores_kernel(
                 out=out[2 * P * k : 2 * P * (k + 1), QH * h : QH * (h + 1)].rearrange("(i p) n -> p i n", p=P),
                 in_=res[:])
 
+        for h in range(2):
+            x_codes[1, h] = held([P, QH], U32, "x_codes1%d" % h)[:]
+        late0 = keep.tile([P, QH], U32, name="late0", tag="wg1", align_bytes=64)
+        gather_v2(1, 0, late0[:])
+        quantise_x(1, 0)
+        late1 = keep.tile([P, QH], U32, name="late1", tag="x_woven10", align_bytes=64)
+        gather_v2(1, 1, late1[:])
+        quantise_x(1, 1)
+        late2 = keep.tile([P, 4 * QH], U32, name="late2", tag="x_woven11", align_bytes=64)
+        for k in range(2, 4):
+            for a in range(2):
+                j = 2 * (k - 2) + a
+                gather_v2(a, k, late2[:, QH * j : QH * (j + 1)])
         n = 0
-        for k in range(4):
-            if not EARLY_A0:
-                gather_v2(0, k)
-            gather_v2(1, k)
+        for h, k in ((0, 0), (0, 1), (1, 0), (1, 1)):
+            score_pass(accs[h, k], 1, h, k)
+            finish(h, k, n)
+            n = n + 1
+        for k in range(2, 4):
             for h in range(2):
-                if k == 0:
-                    quantise_x(1, h)
-                if not EARLY_A0:
-                    accs[h, k] = bank(4 * (1 - h) + k, [P, 2, QH])
-                    score_pass(accs[h, k], 0, h, k)
+                accs[h, k] = bank(2 * (k - 2) + h, [P, 2, QH])
+                score_pass(accs[h, k], 0, h, k)
                 score_pass(accs[h, k], 1, h, k)
                 finish(h, k, n)
                 n = n + 1

@@ -55,10 +55,10 @@ def tile_list_edited_snippet_scores_kernel(
         v2w = {}
         v2s = held([P, S2], U8, "v2s")
         wgs_n = held([P, S], F32, "wgs_n")
-        wgs_d = held([P, 4, S], F32, "wgs_d")
-        gain_n = held([P, 4], F32, "gain_n")
+        wgs_d = [held([P, 2, S], F32, "wgs_d%d" % u) for u in range(2)]
+        vec_rows = held([P, P], F32, "vec_rows")
+        vec_cols = held([P, 12], F32, "vec_cols")
         gain_d = held([P, 4], F32, "gain_d")
-        cand_t = held([P, 8], F32, "cand_t")
         ident = held([P, P], F32, "ident")
         x_turned = held([P, 4, HALF], BF16, "x_turned")
         x_woven = [[keep.tile([P, QH, 4], BF16, name="x_woven", tag="x_woven%d%d" % (b, h), align_bytes=64)
@@ -102,14 +102,26 @@ def tile_list_edited_snippet_scores_kernel(
             nc.sync.dma_start(out=page[:], in_=rows)
             return page
 
+        def load_wgs_dealt(u):
+            for g in (0, 2, 1, 3):
+                nc.sync.dma_start(
+                    out=wgs_d[u][32 * g : 32 * (g + 1), :, :],
+                    in_=wgs.rearrange("(i t) j -> i t j", t=4)[:, 2 * u : 2 * u + 2, :])
+
+        make_identity(nc, ident[:])
         nc.vector.memset(tabs[:].bitcast(I32), 0)
         nc.vector.memset(w4s[:].bitcast(I32), 0)
+        nc.vector.memset(vec_rows[:], 0.0)
         nc.vector.memset(tab2s[:].bitcast(I32), 0)
         for q in range(4):
             nc.gpsimd.dma_start(
                 out=tabs[32 * q + 4 : 32 * q + 12, :].bitcast(I32),
                 in_=tab_scales[0:2, 4 * q : 4 * q + 4, :].bitcast(I32))
-        make_identity(nc, ident[:])
+        nc.gpsimd.dma_start(out=vec_rows[0:4, :], in_=gain[0:HALF].rearrange("(c p) -> c p", p=P))
+        nc.gpsimd.dma_start(out=vec_rows[4:12, :], in_=cand.rearrange("(c p) -> c p", p=P))
+        vec_turned = bank(7, [P, P])
+        nc.tensor.transpose(vec_turned[:], vec_rows[:], ident[:])
+        nc.scalar.copy(out=vec_cols[:], in_=vec_turned[:, 0:12])
 
         pages = {}
         raws = {}
@@ -129,10 +141,9 @@ def tile_list_edited_snippet_scores_kernel(
                 out=w4s[32 * q : 32 * q + 4, :].bitcast(I32),
                 in_=w4_scales[0, 4 * q : 4 * q + 4, :].bitcast(I32))
         load_words(tabw[2], tab_words[2])
-        with nc.allow_non_contiguous_dma(reason="one gain a partition"):
-            nc.sync.dma_start(out=gain_n[:], in_=gain[0:HALF].rearrange("(c p) -> p c", p=P))
-        nc.sync.dma_start(out=wgs_n[:], in_=wgs)
+        nc.sync.dma_start(out=wgs_n[:, 0:HALF], in_=wgs[:, 0:HALF])
         pages[0] = load_page(0)
+        nc.sync.dma_start(out=wgs_n[:, HALF:S], in_=wgs[:, HALF:S])
         for a in range(2):
             raws[a, 256] = load_w1(a, 256, 256, "rawm%d" % a)
         nc.sync.dma_start(list4[:], offs4)
@@ -146,12 +157,8 @@ def tile_list_edited_snippet_scores_kernel(
         raws[1, 512] = load_w1(1, 512, 512, "rawd1")
         pages[2] = load_page(2)
         nc.sync.dma_start(out=gain_d[:], in_=gain[HALF:H].rearrange("(p t) -> p t", t=4))
-        for g in (0, 2, 1, 3):
-            nc.sync.dma_start(
-                out=wgs_d[32 * g : 32 * (g + 1), :, :], in_=wgs.rearrange("(i t) j -> i t j", t=4))
+        load_wgs_dealt(0)
         pages[3] = load_page(3)
-        with nc.allow_non_contiguous_dma(reason="one offset a partition"):
-            nc.sync.dma_start(out=cand_t[:], in_=cand.rearrange("(c p) -> p c", p=P))
 
         nc.vector.tensor_copy(vw[0][:], tabw[0][:].indirect(list1[:]))
         w1q = {}
@@ -173,12 +180,12 @@ def tile_list_edited_snippet_scores_kernel(
             if c < 4:
                 c0, col = 256 * (c // 2), P * (c % 2)
                 w4c, w4sc = w4w[:, 2 * P * c : 2 * P * (c + 1)], w4s[:, P * c : P * (c + 1)]
-                wg_src, gain_col = wgs_n[:], gain_n[:, c : c + 1]
+                wg_src, gain_col = wgs_n[:], vec_cols[:, c : c + 1]
             else:
                 t = c - 4
                 c0, col = HALF, P * t
                 w4c, w4sc = w4w_d[:, 2 * P * t : 2 * P * (t + 1)], w4s_d[:, P * t : P * (t + 1)]
-                wg_src, gain_col = wgs_d[:, t, :], gain_d[:, t : t + 1]
+                wg_src, gain_col = wgs_d[t // 2][:, t % 2, :], gain_d[:, t : t + 1]
             th = keep.tile([P, S], F32, name="th", tag="th%d" % (c % 2), align_bytes=64)
             wg = keep.tile([P, S], F32, name="wg", tag="wg_%d" % c if c in (2, 4) else "wg%d" % (c % 2), align_bytes=64)
             accs = [bank(2 * (c % 2) + jh, [P, HALF]) for jh in range(2)]
@@ -293,6 +300,8 @@ def tile_list_edited_snippet_scores_kernel(
             if c + 4 < 8:
                 pages[c + 4] = load_page(c + 4)
             if c == 0:
+                load_wgs_dealt(1)
+            if c == 1:
                 load_words(tab2w[0], tab2_words[0])
             if c == 2:
                 load_words(tab2w[1], tab2_words[1])
@@ -316,7 +325,12 @@ def tile_list_edited_snippet_scores_kernel(
             for i in range(2):
                 nc.scalar.activation(
                     out=res[:, i, :], in_=accs[h, k][:, i, :], func=ACT.Sigmoid,
-                    bias=cand_t[:, 2 * k + i : 2 * k + i + 1])
+                    bias=vec_cols[:, 4 + 2 * k + i : 5 + 2 * k + i])
+                if n == 7:
+                    rows = slice(P * (2 * k + i), P * (2 * k + i + 1))
+                    nc.sync.dma_start(out=out[rows, QH * h : QH * (h + 1)], in_=res[:, i, :])
+            if n == 7:
+                return
             nc.sync.dma_start(
                 out=out[2 * P * k : 2 * P * (k + 1), QH * h : QH * (h + 1)].rearrange("(i p) n -> p i n", p=P),
                 in_=res[:])

from contextlib import ExitStack

import concourse.mybir as mybir
from concourse.masks import make_identity

F32 = mybir.dt.float32
BF16 = mybir.dt.bfloat16
U32 = mybir.dt.uint32
I32 = mybir.dt.int32
U16 = mybir.dt.uint16
U8 = mybir.dt.uint8
FP8X4 = mybir.dt.float8_e4m3fn_x4
FP4X4 = mybir.dt.float4_e2m1fn_x4
ACT = mybir.ActivationFunctionType
MULT = mybir.AluOpType.mult

P = 128
K, KA, T, H, S, T2, NQ, T3, S2 = 1536, 1024, 4096, 1024, 1024, 2048, 512, 2048, 1024
FLOPS = 2 * K * H * S + 2 * H * S2 * NQ
HALF = 512
QH = 256


def tile_list_edited_snippet_scores_kernel(
    tc, tab_words, tab_scales, tab2_words, tab2_scales, w1, w4_words, w4_scales,
    gain, page0, wgs, cand, offs, offs2, offs3, offs4, out,
):
    nc = tc.nc
    with ExitStack() as ctx:
        keep = ctx.enter_context(tc.tile_pool(name="keep", bufs=1))
        ring = ctx.enter_context(tc.tile_pool(name="ring", bufs=2))
        psum = ctx.enter_context(tc.psum_pool(name="psum", bufs=1))

        def held(shape, dtype, name):
            return keep.tile(shape, dtype, name=name, align_bytes=64)

        def bank(b, shape):
            return psum.tile(shape, F32, name="bank%d" % b, tag="bank%d" % b)

        list1 = keep.tile([P, S // 16], U16, name="list1")
        list2 = keep.tile([P, S2 // 16], U16, name="list2")
        list3 = keep.tile([P, S // 16], U16, name="list3")
        list4 = keep.tile([P, NQ // 16], U16, name="list4")

        tabw = [held([P, T], U32, "tabw%d" % a) for a in range(3)]
        tabs = held([P, T], U8, "tabs")
        tab2w = [held([P, T3], U32, "tab2w%d" % a) for a in range(2)]
        tab2s = held([P, T3], U8, "tab2s")
        w4w = held([P, 2 * H], U8, "w4w")
        w4s = held([P, H], U8, "w4s")
        w4w_d = held([P, H], U8, "w4w_d")
        w4s_d = held([P, HALF], U8, "w4s_d")
        vw = [held([P, S], U32, "vw%d" % a) for a in range(3)]
        vs = held([P, S], U8, "vs")
        v2w = {}
        v2s = held([P, S2], U8, "v2s")
        wgs_n = held([P, S], F32, "wgs_n")
        wgs_d = [held([P, 2, S], F32, "wgs_d%d" % u) for u in range(2)]
        vec_rows = held([P, P], F32, "vec_rows")
        vec_cols = held([P, 12], F32, "vec_cols")
        gain_d = held([P, 4], F32, "gain_d")
        ident = held([P, P], F32, "ident")
        x_turned = held([P, 4, HALF], BF16, "x_turned")
        x_woven = [[keep.tile([P, QH, 4], BF16, name="x_woven", tag="x_woven%d%d" % (b, h), align_bytes=64)
                    for h in range(2)] for b in range(2)]
        x_codes = {}
        x_scales = [[held([P, QH], U8, "x_scales%d%d" % (b, h)) for h in range(2)] for b in range(2)]

        def load_words(tile, words):
            nc.sync.dma_start(out=tile[:].bitcast(I32), in_=words.rearrange("p t i -> p (t i)").bitcast(I32))

        def load_w1(a, c0, width, tag):
            raw = keep.tile([P, 4, width], F32, name="raw%d_%d" % (a, c0), tag=tag, align_bytes=64)
            nc.sync.dma_start(
                out=raw[:], in_=w1[512 * a : 512 * (a + 1), c0 : c0 + width].rearrange("(p j) c -> p j c", j=4))
            return raw

        def quantise_w1(raw, a, c0, width, dealt):
            grouped = ring.tile([P, 4 * width], BF16, name="grouped", tag="grouped", align_bytes=64)
            if dealt is not None:
                nc.scalar.copy(
                    out=grouped[:].rearrange("p (t m j) -> p m t j", t=4, j=4),
                    in_=raw[:].rearrange("p j (m t) -> p m t j", t=4))
            else:
                nc.scalar.copy(
                    out=grouped[:].rearrange("p (c i j) -> p c j i", i=4, j=4),
                    in_=raw[:].rearrange("p j (c i) -> p c j i", i=4))
            if dealt is not None:
                codes = dealt
            else:
                codes = held([P, width], U32, "w1c%d_%d" % (a, c0))[:]
            scales = held([P, width], U8, "w1s%d_%d" % (a, c0))
            nc.vector.quantize_mx(out=codes.bitcast(FP8X4), scales=scales[:], in_=grouped[:])
            return codes, scales

        def load_page(c):
            page = ring.tile([P, T2], F32, name="page", tag="page", bufs=4)
            if c < 4:
                rows = page0[P * c : P * (c + 1), :]
            else:
                rows = page0[HALF:H, :].rearrange("(p t) s -> p t s", t=4)[:, c - 4, :]
            nc.sync.dma_start(out=page[:], in_=rows)
            return page

        def load_wgs_dealt(u):
            for g in (0, 2, 1, 3):
                nc.sync.dma_start(
                    out=wgs_d[u][32 * g : 32 * (g + 1), :, :],
                    in_=wgs.rearrange("(i t) j -> i t j", t=4)[:, 2 * u : 2 * u + 2, :])

        make_identity(nc, ident[:])
        nc.vector.memset(tabs[:].bitcast(I32), 0)
        nc.vector.memset(w4s[:].bitcast(I32), 0)
        nc.vector.memset(vec_rows[:], 0.0)
        nc.vector.memset(tab2s[:].bitcast(I32), 0)
        for q in range(4):
            nc.gpsimd.dma_start(
                out=tabs[32 * q + 4 : 32 * q + 12, :].bitcast(I32),
                in_=tab_scales[0:2, 4 * q : 4 * q + 4, :].bitcast(I32))
        nc.gpsimd.dma_start(out=vec_rows[0:4, :], in_=gain[0:HALF].rearrange("(c p) -> c p", p=P))
        nc.gpsimd.dma_start(out=vec_rows[4:12, :], in_=cand.rearrange("(c p) -> c p", p=P))
        vec_turned = bank(7, [P, P])
        nc.tensor.transpose(vec_turned[:], vec_rows[:], ident[:])
        nc.scalar.copy(out=vec_cols[:], in_=vec_turned[:, 0:12])

        pages = {}
        raws = {}
        load_words(tabw[0], tab_words[0])
        nc.sync.dma_start(list1[:], offs)
        for a in range(2):
            raws[a, 0] = load_w1(a, 0, 256, "rawd%d" % a)
        for q in range(4):
            nc.sync.dma_start(
                out=tabs[32 * q : 32 * q + 4, :].bitcast(I32),
                in_=tab_scales[2, 4 * q : 4 * q + 4, :].bitcast(I32))
        load_words(tabw[1], tab_words[1])
        nc.sync.dma_start(out=w4w[:].bitcast(I32), in_=w4_words[0].bitcast(I32))
        nc.sync.dma_start(list3[:], offs3)
        for q in range(4):
            nc.sync.dma_start(
                out=w4s[32 * q : 32 * q + 4, :].bitcast(I32),
                in_=w4_scales[0, 4 * q : 4 * q + 4, :].bitcast(I32))
        load_words(tabw[2], tab_words[2])
        nc.sync.dma_start(out=wgs_n[:, 0:HALF], in_=wgs[:, 0:HALF])
        pages[0] = load_page(0)
        nc.sync.dma_start(out=wgs_n[:, HALF:S], in_=wgs[:, HALF:S])
        for a in range(2):
            raws[a, 256] = load_w1(a, 256, 256, "rawm%d" % a)
        nc.sync.dma_start(list4[:], offs4)
        pages[1] = load_page(1)
        nc.sync.dma_start(list2[:], offs2)
        for q in range(4):
            nc.sync.dma_start(
                out=tab2s[32 * q : 32 * q + 8, :].bitcast(I32),
                in_=tab2_scales[0:2, 4 * q : 4 * q + 4, :].bitcast(I32))
        raws[0, 512] = load_w1(0, 512, 512, "rawd0")
        raws[1, 512] = load_w1(1, 512, 512, "rawd1")
        pages[2] = load_page(2)
        nc.sync.dma_start(out=gain_d[:], in_=gain[HALF:H].rearrange("(p t) -> p t", t=4))
        load_wgs_dealt(0)
        pages[3] = load_page(3)

        nc.vector.tensor_copy(vw[0][:], tabw[0][:].indirect(list1[:]))
        w1q = {}
        for a in range(2):
            w1q[a, 0] = quantise_w1(raws[a, 0], a, 0, 256, None)
        nc.vector.tensor_copy(vs[:], tabs[:].indirect(list1[:]))
        nc.vector.tensor_copy(vw[1][:], tabw[1][:].indirect(list1[:]))
        for jh in range(2):
            nc.vector.tensor_copy(
                vw[2][:, HALF * jh : HALF * (jh + 1)], tabw[2][:].indirect(list1[:, 32 * jh : 32 * (jh + 1)]))
        nc.vector.tensor_copy(
            out=w4w_d[:].rearrange("p (t m e) -> p m t e", t=4, e=2),
            in_=w4w[:, H : 2 * H].rearrange("p (m t e) -> p m t e", t=4, e=2))
        nc.vector.tensor_copy(
            out=w4s_d[:].rearrange("p (t m) -> p m t", t=4),
            in_=w4s[:, HALF:H].rearrange("p (m t) -> p m t", t=4))

        def stage1(c):
            if c < 4:
                c0, col = 256 * (c // 2), P * (c % 2)
                w4c, w4sc = w4w[:, 2 * P * c : 2 * P * (c + 1)], w4s[:, P * c : P * (c + 1)]
                wg_src, gain_col = wgs_n[:], vec_cols[:, c : c + 1]
            else:
                t = c - 4
                c0, col = HALF, P * t
                w4c, w4sc = w4w_d[:, 2 * P * t : 2 * P * (t + 1)], w4s_d[:, P * t : P * (t + 1)]
                wg_src, gain_col = wgs_d[t // 2][:, t % 2, :], gain_d[:, t : t + 1]
            th = keep.tile([P, S], F32, name="th", tag="th%d" % (c % 2), align_bytes=64)
            wg = keep.tile([P, S], F32, name="wg", tag="wg_%d" % c if c in (2, 4) else "wg%d" % (c % 2), align_bytes=64)
            accs = [bank(2 * (c % 2) + jh, [P, HALF]) for jh in range(2)]
            for a in range(3):
                for jh in range(2):
                    cols = slice(HALF * jh, HALF * (jh + 1))
                    if a < 2:
                        codes, scales = w1q[a, c0]
                        lhs, lhs_s = codes[:, col : col + P].bitcast(FP8X4), scales[:, col : col + P]
                        plane = 4 * (a + 1)
                    else:
                        lhs, lhs_s = w4c.bitcast(FP4X4), w4sc
                        plane = 0
                    nc.tensor.matmul_mx(
                        out=accs[jh][:], lhsT=lhs, lhsT_scale=lhs_s,
                        rhs=vw[a][:, cols].bitcast(FP8X4), rhs_scale=vs[plane:P, cols],
                        start=(a == 0), stop=(a == 2))
            if c == 0:
                for jh in range(2):
                    cols = slice(HALF * jh, HALF * (jh + 1))
                    nc.scalar.activation(out=th[:, cols], in_=accs[jh][:], func=ACT.Tanh)
                    nc.scalar.activation(out=wg[:, cols], in_=wg_src[:, cols], func=ACT.Copy, scale=gain_col)
            else:
                for jh in range(2):
                    cols = slice(HALF * jh, HALF * (jh + 1))
                    nc.scalar.activation(out=th[:, cols], in_=accs[jh][:], func=ACT.Tanh)
                nc.scalar.activation(out=wg[:], in_=wg_src, func=ACT.Copy, scale=gain_col)
            return th, wg

        def scatter(c, th, wg):
            page = pages[c]
            if c == 0:
                for jh in range(2):
                    cols = slice(HALF * jh, HALF * (jh + 1))
                    nc.vector.tensor_tensor(
                        page[:].indirect(list3[:, 32 * jh : 32 * (jh + 1)]), th[:, cols], wg[:, cols], MULT)
            else:
                nc.vector.tensor_tensor(page[:].indirect(list3[:]), th[:], wg[:], MULT)

        def fetch(c):
            page = pages[c]
            picked = ring.tile([P, NQ], F32, name="picked", tag="picked", bufs=3)
            if c < 7:
                nc.vector.tensor_copy(picked[:], page[:].indirect(list4[:]))
            else:
                for h in range(2):
                    nc.vector.tensor_copy(
                        picked[:, QH * h : QH * (h + 1)], page[:].indirect(list4[:, 16 * h : 16 * (h + 1)]))
            if c < 4:
                turned = bank(4 + c % 2, [P, 4, P])
                for nb in range(4):
                    nc.tensor.transpose(turned[:, nb, :], picked[:, P * nb : P * (nb + 1)], ident[:])
                nc.scalar.activation(out=x_turned[:, :, P * c : P * (c + 1)], in_=turned[:], func=ACT.Abs)
            else:
                for h in range(2):
                    nc.scalar.activation(
                        out=x_woven[1][h][:, :, c - 4], in_=picked[:, QH * h : QH * (h + 1)], func=ACT.Abs)

        def turn_back():
            words = x_turned[:].bitcast(F32)
            for h in range(2):
                back = bank(6 + h, [P, 2, 2, P])
                for i in range(2):
                    for u in range(2):
                        nc.tensor.transpose(back[:, i, u, :], words[:, 2 * h + i, u : 256 : 2], ident[:])
                nc.scalar.copy(
                    out=x_woven[0][h][:].rearrange("p n t -> p (n t)").bitcast(F32).rearrange(
                        "p (i n u) -> p i n u", i=2, u=2),
                    in_=back[:].rearrange("p i u n -> p i n u"))

        def quantise_x(b, h):
            nc.vector.quantize_mx(
                out=x_codes[b, h].bitcast(FP8X4), scales=x_scales[b][h][:],
                in_=x_woven[b][h][:].rearrange("p n t -> p (n t)"))

        def gather_v2(a, k, dst):
            nc.vector.tensor_copy(dst, tab2w[a][:].indirect(list2[:, 16 * k : 16 * (k + 1)]))
            v2w[a, k] = dst

        def score_pass(acc, b, h, k):
            for i in range(2):
                cols = slice(P * (2 * k + i), P * (2 * k + i + 1))
                nc.tensor.matmul_mx(
                    out=acc[:, i, :], lhsT=v2w[b, k][:, P * i : P * (i + 1)].bitcast(FP8X4),
                    lhsT_scale=v2s[4 * b : P, cols],
                    rhs=x_codes[b, h].bitcast(FP8X4), rhs_scale=x_scales[b][h][:],
                    start=(b == 0 and i == 0), stop=(b == 1 and i == 1))

        made = {0: stage1(0), 1: stage1(1)}
        for c in range(8):
            scatter(c, *made[c])
            if c == 0:
                for a in range(2):
                    w1q[a, 256] = quantise_w1(raws[a, 256], a, 256, 256, None)
            if c == 1:
                nc.vector.tensor_copy(v2s[:], tab2s[:].indirect(list2[:]))
            if c == 2:
                dealt_codes = keep.tile([P, 2 * HALF], U32, name="dealt_codes", tag="wg_2", align_bytes=64)
                for a in range(2):
                    w1q[a, HALF] = quantise_w1(
                        raws[a, HALF], a, HALF, HALF, dealt_codes[:, HALF * a : HALF * (a + 1)])
            if c + 2 < 8:
                made[c + 2] = stage1(c + 2)
            if c == 4:
                codes0 = keep.tile([P, NQ], U32, name="codes0", tag="wg_4", align_bytes=64)
                for h in range(2):
                    x_codes[0, h] = codes0[:, QH * h : QH * (h + 1)]
                    quantise_x(0, h)
            fetch(c)
            if c == 3:
                turn_back()
            if c + 4 < 8:
                pages[c + 4] = load_page(c + 4)
            if c == 0:
                load_wgs_dealt(1)
            if c == 1:
                load_words(tab2w[0], tab2_words[0])
            if c == 2:
                load_words(tab2w[1], tab2_words[1])
            if c == 5:
                early = held([P, 2 * QH], U32, "v2_early")
                nc.vector.tensor_copy(early[:], tab2w[0][:].indirect(list2[:, 0:32]))
                for k in range(2):
                    v2w[0, k] = early[:, QH * k : QH * (k + 1)]

        accs = {}
        for h in range(2):
            for k in range(2):
                accs[h, k] = bank(4 + 2 * h + k, [P, 2, QH])
                score_pass(accs[h, k], 0, h, k)
        out_tags = [(keep, "th0"), (keep, "wg0"), (keep, "rawd0"), (keep, "rawd1"),
                    (ring, "grouped"), (ring, "grouped"), (keep, "rawm0"), (keep, "rawm1")]

        def finish(h, k, n):
            pool, tag = out_tags[n]
            res = pool.tile([P, 2, QH], F32, name="res", tag=tag, align_bytes=64)
            for i in range(2):
                nc.scalar.activation(
                    out=res[:, i, :], in_=accs[h, k][:, i, :], func=ACT.Sigmoid,
                    bias=vec_cols[:, 4 + 2 * k + i : 5 + 2 * k + i])
                if n == 7:
                    rows = slice(P * (2 * k + i), P * (2 * k + i + 1))
                    nc.sync.dma_start(out=out[rows, QH * h : QH * (h + 1)], in_=res[:, i, :])
            if n == 7:
                return
            nc.sync.dma_start(
                out=out[2 * P * k : 2 * P * (k + 1), QH * h : QH * (h + 1)].rearrange("(i p) n -> p i n", p=P),
                in_=res[:])

        for h in range(2):
            x_codes[1, h] = held([P, QH], U32, "x_codes1%d" % h)[:]
        late0 = keep.tile([P, QH], U32, name="late0", tag="wg1", align_bytes=64)
        gather_v2(1, 0, late0[:])
        quantise_x(1, 0)
        late1 = keep.tile([P, QH], U32, name="late1", tag="x_woven10", align_bytes=64)
        gather_v2(1, 1, late1[:])
        quantise_x(1, 1)
        late2 = keep.tile([P, 4 * QH], U32, name="late2", tag="x_woven11", align_bytes=64)
        for k in range(2, 4):
            for a in range(2):
                j = 2 * (k - 2) + a
                gather_v2(a, k, late2[:, QH * j : QH * (j + 1)])
        n = 0
        for h, k in ((0, 0), (0, 1), (1, 0), (1, 1)):
            score_pass(accs[h, k], 1, h, k)
            finish(h, k, n)
            n = n + 1
        for k in range(2, 4):
            for h in range(2):
                accs[h, k] = bank(2 * (k - 2) + h, [P, 2, QH])
                score_pass(accs[h, k], 0, h, k)
                score_pass(accs[h, k], 1, h, k)
                finish(h, k, n)
                n = n + 1
